import numpy as np
import ml_dtypes


def mxq(x, axis, fmt="e4m3"):
    dtype, down = {"e4m3": (ml_dtypes.float8_e4m3fn, 7), "e5m2": (ml_dtypes.float8_e5m2, 14)}[fmt]
    v = np.moveaxis(np.asarray(x, np.float32).astype(ml_dtypes.bfloat16).astype(np.float64), axis, -1)
    blocks = v.reshape(v.shape[:-1] + (-1, 32))
    amax = np.abs(blocks).max(-1, keepdims=True)
    byte = np.maximum(np.where(amax > 0, np.frexp(amax)[1] - 1 + 127, 0) - down, 1)
    scale = np.exp2(byte - 127.0)
    codes = (blocks / scale).astype(np.float32).astype(dtype).astype(np.float64)
    return np.moveaxis((codes * scale).reshape(v.shape), -1, axis)


WIDE = False


def mx_kscale(k):
    if not WIDE:
        return np.ones(k)
    levels = np.array([10, -10, 5, -5, 0])
    if k % 512:
        return np.exp2(np.random.permutation(np.resize(levels, k // 32))).repeat(32)
    a = np.empty((k // 512, 16))
    for p in range(k // 512):
        a[p, :8] = np.random.permutation(np.resize(levels, 8))
        for g in range(8):
            far = levels[np.abs(levels - a[p, g]) >= 10]
            a[p, g + 8] = far[np.random.randint(len(far))]
    return np.exp2(a.ravel()).repeat(32)


def f64(x):
    return np.asarray(x).astype(np.float64)


def striped(idx):
    return np.tile(idx.reshape(-1, 16).T, (8, 1)).astype(np.uint16)


def unstriped(offs):
    return offs[:16].T.reshape(-1).astype(np.int64)


def pack_weight(w):
    k, n = w.shape
    w = f64(np.asarray(w, np.float32).astype(ml_dtypes.bfloat16)).reshape(k // 32, 32, n)
    amax = np.abs(w).max(1)
    byte = np.clip(np.where(amax > 0, np.frexp(amax)[1] - 1 + 127 - 7, 1), 1, 254)
    scaled = (w * np.exp2(127.0 - byte)[:, None, :]).reshape(k, n).astype(np.float32)
    words = np.ascontiguousarray(scaled.reshape(k // 512, 128, 4, n).transpose(0, 1, 3, 2)).astype(ml_dtypes.float8_e4m3fn).view(np.uint8)
    return words, np.ascontiguousarray(byte.astype(np.uint8).reshape(k // 512, 16, n))


def unpack_weight(words, scales):
    g, p, n, _ = words.shape
    vals = np.ascontiguousarray(words).view(ml_dtypes.float8_e4m3fn).astype(np.float64) * np.repeat(np.exp2(scales.astype(np.float64) - 127.0), 8, axis=1)[..., None]
    return vals.transpose(0, 1, 3, 2).reshape(g * 512, n)


def relu(v):
    return np.maximum(v, 0.0)


K, T, S, N = 1024, 2048, 1024, 512


def setup_inputs():
    n = np.random.standard_normal
    s = mx_kscale(K)[:, None]
    words, scales = pack_weight(n((K, N)) / np.sqrt(K) / s)
    return {
        "xT": (n((K, T)) * s).astype(np.float32),
        "w_words": words,
        "w_scales": scales,
        "b": (0.3 * n((N, 1))).astype(np.float32),
        "offs": striped(np.sort(np.random.permutation(T)[:S])),
    }


def reference(xT, w_words, w_scales, b, offs):
    w = unpack_weight(w_words, w_scales)
    idx = unstriped(offs)
    xq = mxq(f64(xT)[:, idx], 0, "e4m3")
    y = w.T @ xq
    y = relu(y + f64(b))
    return y

@@ -1,0 +1,147 @@
+from contextlib import ExitStack
+
+import concourse.mybir as mybir
+
+K, T, S, N = 1024, 2048, 1024, 512
+FLOPS = 2 * K * S * N
+BYTES = 4 * K * T + K * N + K * N // 32 + 4 * N + 2 * 8 * S * 2 + 4 * N * S
+
+F32 = mybir.dt.float32
+BF16 = mybir.dt.bfloat16
+I32 = mybir.dt.int32
+U32 = mybir.dt.uint32
+U16 = mybir.dt.uint16
+U8 = mybir.dt.uint8
+FP8X4 = mybir.dt.float8_e4m3fn_x4
+RELU = mybir.ActivationFunctionType.Relu
+ADD, MAX = mybir.AluOpType.add, mybir.AluOpType.max
+
+P = 128
+PASSES = 2
+MT = N // P
+CH = 256
+NCH = S // CH
+EDGES = [S + CH, S + 2 * CH, S + 3 * CH, T]
+
+
+def tile_picked_pick_lin_relu_srt_e_kernel(tc, xT, w_words, w_scales, b, offs, out):
+    nc = tc.nc
+    with ExitStack() as ctx:
+        keep = ctx.enter_context(tc.tile_pool(name="keep", bufs=1))
+        psum = ctx.enter_context(tc.psum_pool(name="psum", bufs=2))
+
+        list_tile = keep.tile([P, S // 16], U16, name="list_tile")
+        nc.sync.dma_start(list_tile[:], offs)
+
+        w_codes = keep.tile([P, PASSES, N], I32, name="w_codes", align_bytes=64)
+        w_planes = keep.tile([P, PASSES, N], U8, name="w_planes", align_bytes=64)
+        bias = keep.tile([P, MT, 1], F32, name="bias")
+        nc.vector.memset(w_planes[:].rearrange("p a m -> p (a m)").bitcast(I32), 0)
+        for q in range(4):
+            nc.scalar.dma_start(
+                w_planes[32 * q : 32 * q + 4, :, :].bitcast(I32),
+                w_scales[:, 4 * q : 4 * q + 4, :].rearrange("a q m -> q a m").bitcast(I32),
+            )
+        with nc.allow_non_contiguous_dma(reason="512 bias values, once"):
+            nc.scalar.dma_start(bias[:], b.rearrange("(c p) o -> p c o", p=P))
+
+        x_view = xT.rearrange("(a p u j) t -> a u p j t", a=PASSES, u=2, j=2)
+        raw = [[keep.tile([P, 2, T], F32, name=f"raw{a}{u}") for u in range(2)] for a in range(PASSES)]
+        pairs = [[keep.tile([P, T, 2], BF16, name=f"pairs{a}{u}") for u in range(2)] for a in range(PASSES)]
+        grouped = [keep.tile([P, S, 4], BF16, name=f"grouped{a}", align_bytes=64) for a in range(PASSES)]
+        codes = [keep.tile([P, S], U32, name=f"codes{a}", align_bytes=64) for a in range(PASSES)]
+        planes = [keep.tile([P, S], U8, name=f"planes{a}", align_bytes=64) for a in range(PASSES)]
+
+        def load(a, u, t0, t1):
+            nc.sync.dma_start(raw[a][u][:, :, t0:t1], x_view[a, u, :, :, t0:t1])
+
+        def load_w(a):
+            nc.sync.dma_start(w_codes[:, a, :], w_words[a].rearrange("p m r -> p (m r)").bitcast(I32))
+
+        def round_pairs(a, u, t0, t1, cut):
+            for eng, lo, hi in ((nc.scalar.copy, t0, cut), (nc.vector.tensor_copy, cut, t1)):
+                eng(pairs[a][u][:, lo:hi, :], raw[a][u][:, :, lo:hi].rearrange("p j t -> p t j"))
+
+        def gather(a, u, c0, c1, window):
+            words = pairs[a][u][:].rearrange("p t j -> p (t j)").bitcast(U32)
+            picked = grouped[a][:].rearrange("p s r -> p (s r)").bitcast(U32)
+            nc.vector.tensor_copy(
+                picked[:, 2 * c0 + u : 2 * c1 : 2],
+                words[:, 0:window].indirect(list_tile[:, c0 // 16 : c1 // 16]),
+            )
+
+        def quantize(a, c0, c1):
+            nc.vector.quantize_mx(
+                out=codes[a][:, c0:c1].bitcast(FP8X4),
+                scales=planes[a][:, c0:c1],
+                in_=grouped[a][:].rearrange("p s r -> p (s r)")[:, 4 * c0 : 4 * c1],
+            )
+
+        acc = {}
+
+        def multiply(a, c):
+            for m in range(MT):
+                if a == 0:
+                    acc[c, m] = psum.tile([P, CH], F32, name=f"acc{m}")
+                cols = slice(c * CH, (c + 1) * CH)
+                rows = slice(m * P, (m + 1) * P)
+                nc.tensor.matmul_mx(
+                    out=acc[c, m][:],
+                    lhsT=w_codes[:, a, rows].bitcast(FP8X4),
+                    lhsT_scale=w_planes[:, a, rows],
+                    rhs=codes[a][:, cols].bitcast(FP8X4),
+                    rhs_scale=planes[a][:, cols],
+                    start=(a == 0),
+                    stop=(a == PASSES - 1),
+                )
+
+        out_view = out.rearrange("(m p) s -> p m s", p=P)
+
+        def finish(c):
+            y = keep.tile([P, MT, CH], F32, name=f"y{c}")
+            cols = slice(c * CH, (c + 1) * CH)
+            for m in range(MT):
+                if m < 2:
+                    nc.scalar.activation(y[:, m, :], acc[c, m][:], RELU, bias=bias[:, m, :])
+                else:
+                    nc.vector.tensor_scalar(y[:, m, :], acc[c, m][:], bias[:, m, :], 0.0, op0=ADD, op1=MAX)
+            for h in range(2):
+                nc.sync.dma_start(out_view[:, 2 * h : 2 * h + 2, cols], y[:, 2 * h : 2 * h + 2, :])
+
+        HALF = T // 2
+        load(0, 0, 0, HALF)
+        load(0, 0, HALF, T)
+        load(0, 1, 0, HALF)
+        load(0, 1, HALF, T)
+        load_w(0)
+        load_w(1)
+        load(1, 0, 0, HALF)
+        load(1, 0, HALF, T)
+        starts = [0] + EDGES[:-1]
+        for t0, t1 in zip(starts, EDGES):
+            load(1, 1, t0, t1)
+
+        for a, u in ((0, 0), (0, 1), (1, 0)):
+            round_pairs(a, u, 0, HALF, 640)
+            round_pairs(a, u, HALF, T, HALF + 640)
+            gather(a, u, 0, S, T)
+            if u == 1:
+                for h in range(2):
+                    quantize(a, h * S // 2, (h + 1) * S // 2)
+                multiply(0, 0)
+                multiply(0, 1)
+
+        def prepare(c):
+            cut = 800 if c == 0 else starts[c] + 128
+            round_pairs(1, 1, starts[c], EDGES[c], cut)
+            gather(1, 1, c * CH, (c + 1) * CH, EDGES[c])
+            quantize(1, c * CH, (c + 1) * CH)
+
+        prepare(0)
+        for c in range(NCH):
+            multiply(1, c)
+            if c + 1 < NCH:
+                prepare(c + 1)
+            finish(c)
+            if c + 2 < NCH:
+                multiply(0, c + 2)

@@ -1,6 +1,7 @@
 from contextlib import ExitStack
 
 import concourse.mybir as mybir
+from concourse.masks import make_identity
 
 K, T, S, N = 1024, 2048, 1024, 512
 FLOPS = 2 * K * S * N
@@ -21,7 +22,22 @@ PASSES = 2
 MT = N // P
 CH = 256
 NCH = S // CH
-EDGES = [S + CH, S + 2 * CH, S + 3 * CH, T]
+PIECES = [
+    (0, 0, 0, 512, 360),
+    (0, 0, 512, 1024, 872),
+    (0, 0, 1024, 2048, 1744),
+    (0, 1, 0, 1024, 616),
+    (0, 1, 1024, 2048, 1640),
+    (1, 0, 0, 1024, 616),
+    (1, 0, 1024, 2048, 1792),
+    (1, 1, 0, 1024, 616),
+    (1, 1, 1024, 1280, 1216),
+    (1, 1, 1280, 1536, 1536),
+    (1, 1, 1536, 1792, 1792),
+    (1, 1, 1792, 2048, 1944),
+]
+SCALAR_M = ((0, 1, 2), (0, 1, 2), (0, 1, 2), (0, 2))
+STORE = (2, 2, 2, 1)
 
 
 def tile_picked_pick_lin_relu_srt_e_kernel(tc, xT, w_words, w_scales, b, offs, out):
@@ -35,19 +51,22 @@ def tile_picked_pick_lin_relu_srt_e_kernel(tc, xT, w_words, w_scales, b, offs, o
 
         w_codes = keep.tile([P, PASSES, N], I32, name="w_codes", align_bytes=64)
         w_planes = keep.tile([P, PASSES, N], U8, name="w_planes", align_bytes=64)
-        bias = keep.tile([P, MT, 1], F32, name="bias")
         nc.vector.memset(w_planes[:].rearrange("p a m -> p (a m)").bitcast(I32), 0)
+        bias_rows = keep.tile([P, P], F32, name="bias_rows")
+        nc.vector.memset(bias_rows[:], 0.0)
+        nc.scalar.dma_start(bias_rows[0:MT, :], b.rearrange("(c p) o -> c (p o)", p=P))
         for q in range(4):
             nc.scalar.dma_start(
                 w_planes[32 * q : 32 * q + 4, :, :].bitcast(I32),
                 w_scales[:, 4 * q : 4 * q + 4, :].rearrange("a q m -> q a m").bitcast(I32),
             )
-        with nc.allow_non_contiguous_dma(reason="512 bias values, once"):
-            nc.scalar.dma_start(bias[:], b.rearrange("(c p) o -> p c o", p=P))
+        ident = keep.tile([P, P], F32, name="ident")
+        make_identity(nc, ident[:])
 
         x_view = xT.rearrange("(a p u j) t -> a u p j t", a=PASSES, u=2, j=2)
         raw = [[keep.tile([P, 2, T], F32, name=f"raw{a}{u}") for u in range(2)] for a in range(PASSES)]
         pairs = [[keep.tile([P, T, 2], BF16, name=f"pairs{a}{u}") for u in range(2)] for a in range(PASSES)]
+        picked = [keep.tile([P, 2, S], U32, name=f"picked{a}") for a in range(PASSES)]
         grouped = [keep.tile([P, S, 4], BF16, name=f"grouped{a}", align_bytes=64) for a in range(PASSES)]
         codes = [keep.tile([P, S], U32, name=f"codes{a}", align_bytes=64) for a in range(PASSES)]
         planes = [keep.tile([P, S], U8, name=f"planes{a}", align_bytes=64) for a in range(PASSES)]
@@ -60,14 +79,17 @@ def tile_picked_pick_lin_relu_srt_e_kernel(tc, xT, w_words, w_scales, b, offs, o
 
         def round_pairs(a, u, t0, t1, cut):
             for eng, lo, hi in ((nc.scalar.copy, t0, cut), (nc.vector.tensor_copy, cut, t1)):
-                eng(pairs[a][u][:, lo:hi, :], raw[a][u][:, :, lo:hi].rearrange("p j t -> p t j"))
+                if lo < hi:
+                    eng(pairs[a][u][:, lo:hi, :], raw[a][u][:, :, lo:hi].rearrange("p j t -> p t j"))
 
-        def gather(a, u, c0, c1, window):
+        def gather(a, u, c0, c1):
             words = pairs[a][u][:].rearrange("p t j -> p (t j)").bitcast(U32)
-            picked = grouped[a][:].rearrange("p s r -> p (s r)").bitcast(U32)
+            nc.vector.tensor_copy(picked[a][:, u, c0:c1], words[:, 0 : S + c1].indirect(list_tile[:, c0 // 16 : c1 // 16]))
+
+        def weave(a, c0, c1):
             nc.vector.tensor_copy(
-                picked[:, 2 * c0 + u : 2 * c1 : 2],
-                words[:, 0:window].indirect(list_tile[:, c0 // 16 : c1 // 16]),
+                grouped[a][:, c0:c1, :].rearrange("p s (u j) -> p s u j", u=2),
+                picked[a][:, :, c0:c1].bitcast(BF16).rearrange("p u (s j) -> p s u j", j=2),
             )
 
         def quantize(a, c0, c1):
@@ -96,52 +118,49 @@ def tile_picked_pick_lin_relu_srt_e_kernel(tc, xT, w_words, w_scales, b, offs, o
                 )
 
         out_view = out.rearrange("(m p) s -> p m s", p=P)
+        bias = keep.tile([P, MT], F32, name="bias")
+
+        def make_bias():
+            turned = psum.tile([P, P], F32, name="turned", tag="acc0")
+            nc.tensor.transpose(turned[:], bias_rows[:], ident[:])
+            nc.scalar.copy(bias[:], turned[:, 0:MT])
 
         def finish(c):
             y = keep.tile([P, MT, CH], F32, name=f"y{c}")
             cols = slice(c * CH, (c + 1) * CH)
             for m in range(MT):
-                if m < 2:
-                    nc.scalar.activation(y[:, m, :], acc[c, m][:], RELU, bias=bias[:, m, :])
+                if m in SCALAR_M[c]:
+                    nc.scalar.activation(y[:, m, :], acc[c, m][:], RELU, bias=bias[:, m : m + 1])
                 else:
-                    nc.vector.tensor_scalar(y[:, m, :], acc[c, m][:], bias[:, m, :], 0.0, op0=ADD, op1=MAX)
-            for h in range(2):
-                nc.sync.dma_start(out_view[:, 2 * h : 2 * h + 2, cols], y[:, 2 * h : 2 * h + 2, :])
+                    nc.vector.tensor_scalar(y[:, m, :], acc[c, m][:], bias[:, m : m + 1], 0.0, op0=ADD, op1=MAX)
+            for m in range(0, MT, STORE[c]):
+                nc.sync.dma_start(out_view[:, m : m + STORE[c], cols], y[:, m : m + STORE[c], :])
 
-        HALF = T // 2
-        load(0, 0, 0, HALF)
-        load(0, 0, HALF, T)
-        load(0, 1, 0, HALF)
-        load(0, 1, HALF, T)
-        load_w(0)
-        load_w(1)
-        load(1, 0, 0, HALF)
-        load(1, 0, HALF, T)
-        starts = [0] + EDGES[:-1]
-        for t0, t1 in zip(starts, EDGES):
-            load(1, 1, t0, t1)
-
-        for a, u in ((0, 0), (0, 1), (1, 0)):
-            round_pairs(a, u, 0, HALF, 640)
-            round_pairs(a, u, HALF, T, HALF + 640)
-            gather(a, u, 0, S, T)
-            if u == 1:
-                for h in range(2):
-                    quantize(a, h * S // 2, (h + 1) * S // 2)
-                multiply(0, 0)
-                multiply(0, 1)
-
-        def prepare(c):
-            cut = 800 if c == 0 else starts[c] + 128
-            round_pairs(1, 1, starts[c], EDGES[c], cut)
-            gather(1, 1, c * CH, (c + 1) * CH, EDGES[c])
-            quantize(1, c * CH, (c + 1) * CH)
-
-        prepare(0)
-        for c in range(NCH):
-            multiply(1, c)
-            if c + 1 < NCH:
-                prepare(c + 1)
-            finish(c)
-            if c + 2 < NCH:
-                multiply(0, c + 2)
+        make_bias()
+        for i, (a, u, t0, t1, cut) in enumerate(PIECES):
+            load(a, u, t0, t1)
+            if i == 7:
+                load_w(0)
+                load_w(1)
+        for a, u, t0, t1, cut in PIECES:
+            round_pairs(a, u, t0, t1, cut)
+            if (a, u) != (1, 1):
+                if t1 == T:
+                    gather(a, u, 0, S)
+                    if u == 1:
+                        weave(a, 0, S)
+                        for h in range(2):
+                            quantize(a, h * S // 2, (h + 1) * S // 2)
+                        multiply(0, 0)
+                        multiply(0, 1)
+            elif t1 > S:
+                c = (t1 - S) // CH - 1
+                gather(a, u, c * CH, (c + 1) * CH)
+                weave(a, c * CH, (c + 1) * CH)
+                quantize(a, c * CH, (c + 1) * CH)
+                if c >= 2:
+                    multiply(0, c)
+                multiply(1, c)
+                if c > 0:
+                    finish(c - 1)
+        finish(NCH - 1)

from contextlib import ExitStack

import concourse.mybir as mybir
from concourse.masks import make_identity

K, T, S, N = 1024, 2048, 1024, 512
FLOPS = 2 * K * S * N
BYTES = 4 * K * T + K * N + K * N // 32 + 4 * N + 2 * 8 * S * 2 + 4 * N * S

F32 = mybir.dt.float32
BF16 = mybir.dt.bfloat16
I32 = mybir.dt.int32
U32 = mybir.dt.uint32
U16 = mybir.dt.uint16
U8 = mybir.dt.uint8
FP8X4 = mybir.dt.float8_e4m3fn_x4
RELU = mybir.ActivationFunctionType.Relu
ADD, MAX = mybir.AluOpType.add, mybir.AluOpType.max

P = 128
PASSES = 2
MT = N // P
CH = 256
NCH = S // CH
PIECES = [
    (0, 0, 0, 512, 360),
    (0, 0, 512, 1024, 872),
    (0, 0, 1024, 2048, 1744),
    (0, 1, 0, 1024, 616),
    (0, 1, 1024, 2048, 1640),
    (1, 0, 0, 1024, 616),
    (1, 0, 1024, 2048, 1792),
    (1, 1, 0, 1024, 616),
    (1, 1, 1024, 1280, 1216),
    (1, 1, 1280, 1536, 1536),
    (1, 1, 1536, 1792, 1792),
    (1, 1, 1792, 2048, 1944),
]
SCALAR_M = ((0, 1, 2), (0, 1, 2), (0, 1, 2), (0, 2))
STORE = (2, 2, 2, 1)


def tile_picked_pick_lin_relu_srt_e_kernel(tc, xT, w_words, w_scales, b, offs, out):
    nc = tc.nc
    with ExitStack() as ctx:
        keep = ctx.enter_context(tc.tile_pool(name="keep", bufs=1))
        psum = ctx.enter_context(tc.psum_pool(name="psum", bufs=2))

        list_tile = keep.tile([P, S // 16], U16, name="list_tile")
        nc.sync.dma_start(list_tile[:], offs)

        w_codes = keep.tile([P, PASSES, N], I32, name="w_codes", align_bytes=64)
        w_planes = keep.tile([P, PASSES, N], U8, name="w_planes", align_bytes=64)
        nc.vector.memset(w_planes[:].rearrange("p a m -> p (a m)").bitcast(I32), 0)
        bias_rows = keep.tile([P, P], F32, name="bias_rows")
        nc.vector.memset(bias_rows[:], 0.0)
        nc.scalar.dma_start(bias_rows[0:MT, :], b.rearrange("(c p) o -> c (p o)", p=P))
        for q in range(4):
            nc.scalar.dma_start(
                w_planes[32 * q : 32 * q + 4, :, :].bitcast(I32),
                w_scales[:, 4 * q : 4 * q + 4, :].rearrange("a q m -> q a m").bitcast(I32),
            )
        ident = keep.tile([P, P], F32, name="ident")
        make_identity(nc, ident[:])

        x_view = xT.rearrange("(a p u j) t -> a u p j t", a=PASSES, u=2, j=2)
        raw = [[keep.tile([P, 2, T], F32, name=f"raw{a}{u}") for u in range(2)] for a in range(PASSES)]
        pairs = [[keep.tile([P, T, 2], BF16, name=f"pairs{a}{u}") for u in range(2)] for a in range(PASSES)]
        picked = [keep.tile([P, 2, S], U32, name=f"picked{a}") for a in range(PASSES)]
        grouped = [keep.tile([P, S, 4], BF16, name=f"grouped{a}", align_bytes=64) for a in range(PASSES)]
        codes = [keep.tile([P, S], U32, name=f"codes{a}", align_bytes=64) for a in range(PASSES)]
        planes = [keep.tile([P, S], U8, name=f"planes{a}", align_bytes=64) for a in range(PASSES)]

        def load(a, u, t0, t1):
            nc.sync.dma_start(raw[a][u][:, :, t0:t1], x_view[a, u, :, :, t0:t1])

        def load_w(a):
            nc.sync.dma_start(w_codes[:, a, :], w_words[a].rearrange("p m r -> p (m r)").bitcast(I32))

        def round_pairs(a, u, t0, t1, cut):
            for eng, lo, hi in ((nc.scalar.copy, t0, cut), (nc.vector.tensor_copy, cut, t1)):
                if lo < hi:
                    eng(pairs[a][u][:, lo:hi, :], raw[a][u][:, :, lo:hi].rearrange("p j t -> p t j"))

        def gather(a, u, c0, c1):
            words = pairs[a][u][:].rearrange("p t j -> p (t j)").bitcast(U32)
            nc.vector.tensor_copy(picked[a][:, u, c0:c1], words[:, 0 : S + c1].indirect(list_tile[:, c0 // 16 : c1 // 16]))

        def weave(a, c0, c1):
            nc.vector.tensor_copy(
                grouped[a][:, c0:c1, :].rearrange("p s (u j) -> p s u j", u=2),
                picked[a][:, :, c0:c1].bitcast(BF16).rearrange("p u (s j) -> p s u j", j=2),
            )

        def quantize(a, c0, c1):
            nc.vector.quantize_mx(
                out=codes[a][:, c0:c1].bitcast(FP8X4),
                scales=planes[a][:, c0:c1],
                in_=grouped[a][:].rearrange("p s r -> p (s r)")[:, 4 * c0 : 4 * c1],
            )

        acc = {}

        def multiply(a, c):
            for m in range(MT):
                if a == 0:
                    acc[c, m] = psum.tile([P, CH], F32, name=f"acc{m}")
                cols = slice(c * CH, (c + 1) * CH)
                rows = slice(m * P, (m + 1) * P)
                nc.tensor.matmul_mx(
                    out=acc[c, m][:],
                    lhsT=w_codes[:, a, rows].bitcast(FP8X4),
                    lhsT_scale=w_planes[:, a, rows],
                    rhs=codes[a][:, cols].bitcast(FP8X4),
                    rhs_scale=planes[a][:, cols],
                    start=(a == 0),
                    stop=(a == PASSES - 1),
                )

        out_view = out.rearrange("(m p) s -> p m s", p=P)
        bias = keep.tile([P, MT], F32, name="bias")

        def make_bias():
            turned = psum.tile([P, P], F32, name="turned", tag="acc0")
            nc.tensor.transpose(turned[:], bias_rows[:], ident[:])
            nc.scalar.copy(bias[:], turned[:, 0:MT])

        def finish(c):
            y = keep.tile([P, MT, CH], F32, name=f"y{c}")
            cols = slice(c * CH, (c + 1) * CH)
            for m in range(MT):
                if m in SCALAR_M[c]:
                    nc.scalar.activation(y[:, m, :], acc[c, m][:], RELU, bias=bias[:, m : m + 1])
                else:
                    nc.vector.tensor_scalar(y[:, m, :], acc[c, m][:], bias[:, m : m + 1], 0.0, op0=ADD, op1=MAX)
            for m in range(0, MT, STORE[c]):
                nc.sync.dma_start(out_view[:, m : m + STORE[c], cols], y[:, m : m + STORE[c], :])

        make_bias()
        for i, (a, u, t0, t1, cut) in enumerate(PIECES):
            load(a, u, t0, t1)
            if i == 7:
                load_w(0)
                load_w(1)
        for a, u, t0, t1, cut in PIECES:
            round_pairs(a, u, t0, t1, cut)
            if (a, u) != (1, 1):
                if t1 == T:
                    gather(a, u, 0, S)
                    if u == 1:
                        weave(a, 0, S)
                        for h in range(2):
                            quantize(a, h * S // 2, (h + 1) * S // 2)
                        multiply(0, 0)
                        multiply(0, 1)
            elif t1 > S:
                c = (t1 - S) // CH - 1
                gather(a, u, c * CH, (c + 1) * CH)
                weave(a, c * CH, (c + 1) * CH)
                quantize(a, c * CH, (c + 1) * CH)
                if c >= 2:
                    multiply(0, c)
                multiply(1, c)
                if c > 0:
                    finish(c - 1)
        finish(NCH - 1)
